import numpy as np
import ml_dtypes


def mxq(x, axis, fmt="e4m3"):
    dtype, down = {"e4m3": (ml_dtypes.float8_e4m3fn, 7), "e5m2": (ml_dtypes.float8_e5m2, 14)}[fmt]
    v = np.moveaxis(np.asarray(x, np.float32).astype(ml_dtypes.bfloat16).astype(np.float64), axis, -1)
    blocks = v.reshape(v.shape[:-1] + (-1, 32))
    amax = np.abs(blocks).max(-1, keepdims=True)
    byte = np.maximum(np.where(amax > 0, np.frexp(amax)[1] - 1 + 127, 0) - down, 1)
    scale = np.exp2(byte - 127.0)
    codes = (blocks / scale).astype(np.float32).astype(dtype).astype(np.float64)
    return np.moveaxis((codes * scale).reshape(v.shape), -1, axis)


WIDE = False


def mx_kscale(k):
    if not WIDE:
        return np.ones(k)
    levels = np.array([10, -10, 5, -5, 0])
    if k % 512:
        return np.exp2(np.random.permutation(np.resize(levels, k // 32))).repeat(32)
    a = np.empty((k // 512, 16))
    for p in range(k // 512):
        a[p, :8] = np.random.permutation(np.resize(levels, 8))
        for g in range(8):
            far = levels[np.abs(levels - a[p, g]) >= 10]
            a[p, g + 8] = far[np.random.randint(len(far))]
    return np.exp2(a.ravel()).repeat(32)


def f64(x):
    return np.asarray(x).astype(np.float64)


def striped8(idx):
    return np.concatenate([x.reshape(-1, 16).T for x in idx]).astype(np.uint16)


def runs(offs, k):
    lists = np.stack([offs[16 * r : 16 * r + 16].T.reshape(-1) for r in range(8)]).astype(np.int64)
    return lists[np.arange(k) % 512 // 64]


def pack_weight(w):
    k, n = w.shape
    w = f64(np.asarray(w, np.float32).astype(ml_dtypes.bfloat16)).reshape(k // 32, 32, n)
    amax = np.abs(w).max(1)
    byte = np.clip(np.where(amax > 0, np.frexp(amax)[1] - 1 + 127 - 7, 1), 1, 254)
    scaled = (w * np.exp2(127.0 - byte)[:, None, :]).reshape(k, n).astype(np.float32)
    words = np.ascontiguousarray(scaled.reshape(k // 512, 128, 4, n).transpose(0, 1, 3, 2)).astype(ml_dtypes.float8_e4m3fn).view(np.uint8)
    return words, np.ascontiguousarray(byte.astype(np.uint8).reshape(k // 512, 16, n))


def unpack_weight(words, scales):
    g, p, n, _ = words.shape
    vals = np.ascontiguousarray(words).view(ml_dtypes.float8_e4m3fn).astype(np.float64) * np.repeat(np.exp2(scales.astype(np.float64) - 127.0), 8, axis=1)[..., None]
    return vals.transpose(0, 1, 3, 2).reshape(g * 512, n)


K, T, S, V, N, H = 512, 2048, 1024, 512, 512, 512


def setup_inputs():
    n = np.random.standard_normal
    s = mx_kscale(K)[:, None]
    u = mx_kscale(H)
    packed_xT = pack_weight(n((K, T)) * s)
    return {
        "x_words": packed_xT[0],
        "x_scales": packed_xT[1],
        "w1": (n((K, H)) / np.sqrt(K) / s).astype(np.float32),
        "gn": (np.random.uniform(0.5, 1.5, (H, 1)) * u[:, None]).astype(np.float32),
        "w2": (n((H, N)) / np.sqrt(H) / u[:, None]).astype(np.float32),
        "offs": striped8(np.random.randint(0, T, (8, S))),
        "n1": striped8(np.stack([np.random.permutation(S) for _ in range(8)])),
        "n2": striped8(np.stack([np.random.permutation(V) for _ in range(8)])),
        "n3": striped8(np.stack([np.random.permutation(V) for _ in range(8)])),
    }


def reference(x_words, x_scales, w1, gn, w2, offs, n1, n2, n3):
    xq = unpack_weight(x_words, x_scales)[np.arange(K)[:, None], runs(offs, K)]
    y = mxq(f64(w1), 0, "e4m3").T @ xq
    ln = y[np.arange(H)[:, None], runs(n1, H)]
    sq = (ln) ** 2
    ms = sq.reshape(H, V, 2).sum(axis=2)
    z = f64(gn) * np.sqrt(ms + 0.1)
    h = mxq(f64(w2), 0, "e4m3").T @ mxq(z, 0, "e4m3")
    ex = np.exp(h)
    return np.log(ex + ex[np.arange(N)[:, None], runs(n2, N)]) - (h[np.arange(N)[:, None], runs(n3, N)])

@@ -1,0 +1,234 @@
+from contextlib import ExitStack
+
+import concourse.mybir as mybir
+
+K, T, S, V, N, H = 512, 2048, 1024, 512, 512, 512
+FLOPS = 2 * K * H * S + 2 * H * N * V
+
+F32 = mybir.dt.float32
+BF16 = mybir.dt.bfloat16
+I32 = mybir.dt.int32
+U32 = mybir.dt.uint32
+U16 = mybir.dt.uint16
+U8 = mybir.dt.uint8
+FP8X4 = mybir.dt.float8_e4m3fn_x4
+ACT = mybir.ActivationFunctionType
+ALU = mybir.AluOpType
+
+P = 128
+PACK = 4
+BANK = 512
+LIST_ROWS = 16
+PAIR_CHUNKS = ((0, 256), (256, 128), (384, 128))
+HALF = V // 2
+SCALAR_TILES = 3
+ORDER = (3, 0, 1, 2)
+
+
+def deal_and_round(engine_copy, grouped, raw, m0, m1):
+    engine_copy(
+        out=grouped[:].rearrange("p (t m j) -> p m j t", t=PACK, j=PACK)[:, m0:m1],
+        in_=raw.rearrange("p j (m t) -> p m j t", t=PACK),
+    )
+
+
+def tile_picked_hashprmslse_none_p_kernel(tc, x_words, x_scales, w1, gn, w2, offs, n1, n2, n3, out):
+    nc = tc.nc
+    with ExitStack() as ctx:
+        keep = ctx.enter_context(tc.tile_pool(name="keep", bufs=1))
+        ring = ctx.enter_context(tc.tile_pool(name="ring", bufs=3))
+        psum = ctx.enter_context(tc.psum_pool(name="psum", bufs=8))
+
+        offs_sb = keep.tile([P, S // LIST_ROWS], U16, name="offs_sb")
+        n1_sb = keep.tile([P, S // LIST_ROWS], U16, name="n1_sb")
+        n2_sb = keep.tile([P, V // LIST_ROWS], U16, name="n2_sb")
+        n3_sb = keep.tile([P, V // LIST_ROWS], U16, name="n3_sb")
+
+        warm = keep.tile([P, 2], F32, name="warm")
+        nc.gpsimd.memset(warm[:, 0:1], 1.0)
+
+        table_scales = keep.tile([P, T], U8, name="table_scales")
+        x_scale_plane = keep.tile([P, S], U8, name="x_scale_plane", align_bytes=64)
+        nc.gpsimd.memset(x_scale_plane[:].bitcast(I32), 0)
+
+        table_words = keep.tile([P, T], I32, name="table_words")
+        w1_raw = [keep.tile([P, PACK, H // 2], F32, name=f"w1_raw{a}") for a in range(2)]
+        w2_raw = [keep.tile([P, 2, N], F32, name=f"w2_raw{a}") for a in range(2)]
+        gn_sb = keep.tile([P, PACK], F32, name="gn_sb")
+
+        nc.sync.dma_start(offs_sb[:], offs)
+        nc.sync.dma_start(
+            table_scales[:].bitcast(I32), x_scales[0].bitcast(I32).unsqueeze(1).to_broadcast([16, 8, T // 4])
+        )
+        nc.sync.dma_start(n1_sb[:], n1)
+        nc.sync.dma_start(n2_sb[:], n2)
+        nc.sync.dma_start(n3_sb[:], n3)
+        nc.sync.dma_start(table_words[:], x_words[0].rearrange("p c r -> p (c r)").bitcast(I32))
+        w1_rows = w1.rearrange("(p j) c -> p j c", j=PACK)
+        for a in range(2):
+            nc.sync.dma_start(w1_raw[a][:], w1_rows[:, :, a * (H // 2) : (a + 1) * (H // 2)])
+        nc.gpsimd.dma_start(gn_sb[:], gn.rearrange("(p t) o -> p (t o)", t=PACK))
+        w2_rows = w2.rearrange("(p j) c -> p j c", j=PACK)
+        for a in range(2):
+            nc.sync.dma_start(w2_raw[a][:], w2_rows[:, 2 * a : 2 * a + 2, :])
+        nc.scalar.activation(warm[:, 1:2], warm[:, 0:1], ACT.Sqrt)
+
+        floor = keep.tile([P, PACK], F32, name="floor")
+        gn_sq = keep.tile([P, PACK], F32, name="gn_sq")
+        nonneg = keep.tile([P, PACK], F32, name="nonneg")
+        gn_sign = keep.tile([P, PACK], F32, name="gn_sign")
+        nc.gpsimd.tensor_tensor(gn_sq[:], gn_sb[:], gn_sb[:], ALU.mult)
+        nc.gpsimd.tensor_scalar(floor[:], gn_sq[:], 0.1, 0.0, ALU.mult, ALU.add)
+        nc.gpsimd.tensor_scalar(nonneg[:], gn_sb[:], 0.0, 2.0, ALU.is_ge, ALU.mult)
+        nc.gpsimd.tensor_scalar(gn_sign[:], nonneg[:], 1.0, -1.0, ALU.mult, ALU.add)
+
+        picked_scales = keep.tile([P, S], U8, name="picked_scales")
+        nc.vector.tensor_copy(picked_scales[:], table_scales[:].indirect(offs_sb[:]))
+        for q in range(4):
+            nc.scalar.dma_start(
+                x_scale_plane[32 * q : 32 * q + 4, :].bitcast(I32),
+                picked_scales[32 * q : 32 * q + 32 : 8, :].bitcast(I32),
+            )
+        x_codes = [keep.tile([P, BANK], U32, name=f"x_codes{a}", align_bytes=64) for a in range(2)]
+        cols = BANK // LIST_ROWS
+        for a in range(2):
+            nc.vector.tensor_copy(
+                x_codes[a][:], table_words[:].bitcast(U32).indirect(offs_sb[:, a * cols : (a + 1) * cols])
+            )
+
+        w1_bf = keep.tile([P, H * PACK], BF16, name="w1_bf", align_bytes=64)
+        deal_and_round(nc.scalar.copy, w1_bf, w1_raw[0][:], 0, 64)
+        deal_and_round(nc.scalar.copy, w1_bf, w1_raw[1][:, :, 0:176], 64, 108)
+        deal_and_round(nc.vector.tensor_copy, w1_bf, w1_raw[1][:, :, 176:256], 108, 128)
+        w1_codes = [keep.tile([P, P], U32, name=f"w1_codes{t}", tag=f"w1_codes{t}", align_bytes=64) for t in range(PACK)]
+        w1_scales = [keep.tile([P, P], U8, name=f"w1_scales{t}", align_bytes=64) for t in range(PACK)]
+        sq = [keep.tile([P, S], F32, name=f"sq{t}") for t in range(PACK)]
+        for t in range(PACK):
+            nc.vector.quantize_mx(
+                out=w1_codes[t][:].bitcast(FP8X4), scales=w1_scales[t][:], in_=w1_bf[:, t * BANK : (t + 1) * BANK]
+            )
+        for t in range(PACK):
+            for a in range(2):
+                y = psum.tile([P, BANK], F32, name="bank")
+                nc.tensor.matmul_mx(
+                    out=y[:],
+                    lhsT=w1_codes[t][:].bitcast(FP8X4),
+                    lhsT_scale=w1_scales[t][:],
+                    rhs=x_codes[a][:].bitcast(FP8X4),
+                    rhs_scale=x_scale_plane[:, a * BANK : (a + 1) * BANK],
+                    start=True,
+                    stop=True,
+                )
+                nc.scalar.activation(
+                    sq[t][:, a * BANK : (a + 1) * BANK], y[:], ACT.Square, scale=gn_sb[:, t : t + 1]
+                )
+
+        w2_signed = keep.tile([P, PACK, N], BF16, name="w2_signed")
+        for j in range(PACK):
+            nc.vector.tensor_scalar(
+                w2_signed[:, j, :], w2_raw[j // 2][:, j % 2, :], gn_sign[:, j : j + 1], None, ALU.mult
+            )
+        w2_bf = keep.tile([P, N * PACK], BF16, name="w2_bf", tag="w1_codes3", align_bytes=64)
+        deal_and_round(nc.scalar.copy, w2_bf, w2_signed[:], 0, 128)
+        w2_codes = keep.tile([P, N], U32, name="w2_codes", align_bytes=64)
+        w2_scales = keep.tile([P, N], U8, name="w2_scales", align_bytes=64)
+
+        h_banks = [psum.tile([P, V], F32, name="bank") for t in range(PACK)]
+        h_sb = [keep.tile([P, V], F32, name=f"h_sb{t}") for t in range(PACK)]
+        ms = {}
+        lined = {}
+        z_bf = {}
+
+        def line_up(c, t):
+            v0, width = PAIR_CHUNKS[c]
+            if (c, t) == (2, 3):
+                lined[c, t] = keep.tile([P, 2 * width], F32, name="lined_last", tag="z_bf1", align_bytes=64)
+            else:
+                lined[c, t] = ring.tile([P, 2 * width], F32, name="lined")
+            c0 = 2 * v0 // LIST_ROWS
+            nc.vector.tensor_copy(lined[c, t][:], sq[t][:].indirect(n1_sb[:, c0 : c0 + 2 * width // LIST_ROWS]))
+
+        def add_pairs(c, t):
+            width = PAIR_CHUNKS[c][1]
+            if t == 0:
+                ms[c] = keep.tile(
+                    [P, PACK, width], F32, name=f"ms{c}", tag="z_bf0" if c == 2 else f"ms{c}", align_bytes=64
+                )
+            pairs = lined[c, t][:].rearrange("p (v e) -> p v e", e=2)
+            nc.vector.scalar_tensor_tensor(
+                ms[c][:, t, :], pairs[:, :, 0], floor[:, t : t + 1], pairs[:, :, 1], ALU.add, ALU.add
+            )
+
+        def root(c):
+            width = PAIR_CHUNKS[c][1]
+            z_bf[c] = keep.tile([P, width * PACK], BF16, name=f"z_bf{c}", tag=f"z_bf{c}", align_bytes=64)
+            nc.scalar.activation(
+                z_bf[c][:].rearrange("p (c i t) -> p c t i", i=4, t=PACK),
+                ms[c][:].rearrange("p t (c i) -> p c t i", i=4),
+                ACT.Sqrt,
+            )
+
+        def second_product(c):
+            v0, width = PAIR_CHUNKS[c]
+            z_codes = keep.tile([P, width], U32, name=f"z_codes{c}", align_bytes=64)
+            z_scales = keep.tile([P, width], U8, name=f"z_scales{c}", align_bytes=64)
+            nc.vector.quantize_mx(out=z_codes[:].bitcast(FP8X4), scales=z_scales[:], in_=z_bf[c][:])
+            for t in ORDER:
+                nc.tensor.matmul_mx(
+                    out=h_banks[t][:, v0 : v0 + width],
+                    lhsT=w2_codes[:, t * P : (t + 1) * P].bitcast(FP8X4),
+                    lhsT_scale=w2_scales[:, t * P : (t + 1) * P],
+                    rhs=z_codes[:].bitcast(FP8X4),
+                    rhs_scale=z_scales[:],
+                    start=True,
+                    stop=True,
+                )
+            copy = nc.scalar.copy if c + 1 < len(PAIR_CHUNKS) else nc.vector.tensor_copy
+            for t in ORDER:
+                copy(h_sb[t][:, v0 : v0 + width], h_banks[t][:, v0 : v0 + width])
+
+        steps = [(c, t) for c in range(len(PAIR_CHUNKS)) for t in range(PACK)]
+        line_up(*steps[0])
+        for now, ahead in zip(steps, steps[1:] + [None]):
+            if ahead == (2, 3):
+                second_product(1)
+            if ahead is not None:
+                line_up(*ahead)
+            if now == (2, 0):
+                nc.vector.quantize_mx(out=w2_codes[:].bitcast(FP8X4), scales=w2_scales[:], in_=w2_bf[:])
+                second_product(0)
+            add_pairs(*now)
+            if now[1] == PACK - 1:
+                root(now[0])
+        second_product(2)
+
+        ex = [keep.tile([P, V], F32, name=f"ex{t}") for t in range(PACK)]
+        ex_n2 = [keep.tile([P, V], F32, name=f"ex_n2_{t}") for t in range(PACK)]
+        h_n3 = [keep.tile([P, V], F32, name=f"h_n3_{t}") for t in range(PACK)]
+        total = [keep.tile([P, V], F32, name=f"total{t}") for t in range(PACK)]
+        half_cols = HALF // LIST_ROWS
+        halves = [(slice(a * HALF, (a + 1) * HALF), slice(a * half_cols, (a + 1) * half_cols)) for a in range(2)]
+        for t in ORDER:
+            nc.scalar.activation(ex[t][:], h_sb[t][:], ACT.Exp)
+            if t < SCALAR_TILES:
+                for v, lc in halves:
+                    nc.scalar.activation(ex_n2[t][:, v], h_sb[t][:].indirect(n2_sb[:, lc]), ACT.Exp)
+
+        def fetch_h(t):
+            for v, lc in halves:
+                nc.vector.tensor_copy(h_n3[t][:, v], h_sb[t][:].indirect(n3_sb[:, lc]))
+
+        fetch_h(3)
+        for v, lc in halves:
+            nc.vector.tensor_copy(ex_n2[3][:, v], ex[3][:].indirect(n2_sb[:, lc]))
+        for now, ahead in zip(ORDER, ORDER[1:] + (None,)):
+            if ahead is not None:
+                fetch_h(ahead)
+            nc.vector.tensor_tensor(total[now][:], ex[now][:], ex_n2[now][:], ALU.add)
+        out_rows = out.rearrange("(p t) v -> p t v", t=PACK)
+        for t in ORDER:
+            lse = ring.tile([P, V], F32, name="lse")
+            nc.scalar.activation(lse[:], total[t][:], ACT.Ln)
+            res = keep.tile([P, V], F32, name=f"res{t}")
+            nc.vector.tensor_tensor(res[:], lse[:], h_n3[t][:], ALU.subtract)
+            nc.sync.dma_start(out_rows[:, t, :], res[:])

@@ -25,10 +25,10 @@ SCALAR_TILES = 3
 ORDER = (3, 0, 1, 2)
 
 
-def deal_and_round(engine_copy, grouped, raw, m0, m1):
+def deal_and_round(engine_copy, grouped, raw, m0, m1, t0=0, t1=PACK):
     engine_copy(
-        out=grouped[:].rearrange("p (t m j) -> p m j t", t=PACK, j=PACK)[:, m0:m1],
-        in_=raw.rearrange("p j (m t) -> p m j t", t=PACK),
+        out=grouped[:].rearrange("p (t m j) -> p m j t", t=PACK, j=PACK)[:, m0:m1, :, t0:t1],
+        in_=raw.rearrange("p j (m t) -> p m j t", t=PACK)[:, :, :, t0:t1],
     )
 
 
@@ -47,13 +47,12 @@ def tile_picked_hashprmslse_none_p_kernel(tc, x_words, x_scales, w1, gn, w2, off
         warm = keep.tile([P, 2], F32, name="warm")
         nc.gpsimd.memset(warm[:, 0:1], 1.0)
 
-        table_scales = keep.tile([P, T], U8, name="table_scales")
+        table_scales = keep.tile([P, T], U8, name="table_scales", tag="table_scales")
         x_scale_plane = keep.tile([P, S], U8, name="x_scale_plane", align_bytes=64)
         nc.gpsimd.memset(x_scale_plane[:].bitcast(I32), 0)
 
         table_words = keep.tile([P, T], I32, name="table_words")
         w1_raw = [keep.tile([P, PACK, H // 2], F32, name=f"w1_raw{a}") for a in range(2)]
-        w2_raw = [keep.tile([P, 2, N], F32, name=f"w2_raw{a}") for a in range(2)]
         gn_sb = keep.tile([P, PACK], F32, name="gn_sb")
 
         nc.sync.dma_start(offs_sb[:], offs)
@@ -68,9 +67,6 @@ def tile_picked_hashprmslse_none_p_kernel(tc, x_words, x_scales, w1, gn, w2, off
         for a in range(2):
             nc.sync.dma_start(w1_raw[a][:], w1_rows[:, :, a * (H // 2) : (a + 1) * (H // 2)])
         nc.gpsimd.dma_start(gn_sb[:], gn.rearrange("(p t) o -> p (t o)", t=PACK))
-        w2_rows = w2.rearrange("(p j) c -> p j c", j=PACK)
-        for a in range(2):
-            nc.sync.dma_start(w2_raw[a][:], w2_rows[:, 2 * a : 2 * a + 2, :])
         nc.scalar.activation(warm[:, 1:2], warm[:, 0:1], ACT.Sqrt)
 
         floor = keep.tile([P, PACK], F32, name="floor")
@@ -85,10 +81,14 @@ def tile_picked_hashprmslse_none_p_kernel(tc, x_words, x_scales, w1, gn, w2, off
         picked_scales = keep.tile([P, S], U8, name="picked_scales")
         nc.vector.tensor_copy(picked_scales[:], table_scales[:].indirect(offs_sb[:]))
         for q in range(4):
-            nc.scalar.dma_start(
+            nc.sync.dma_start(
                 x_scale_plane[32 * q : 32 * q + 4, :].bitcast(I32),
                 picked_scales[32 * q : 32 * q + 32 : 8, :].bitcast(I32),
             )
+        w2_held = keep.tile([P, PACK * N], F32, name="w2_held", tag="table_scales")
+        w2_rows = w2.rearrange("(p j) c -> p (j c)", j=PACK)
+        for a in range(2):
+            nc.sync.dma_start(w2_held[:, 2 * a * N : 2 * (a + 1) * N], w2_rows[:, 2 * a * N : 2 * (a + 1) * N])
         x_codes = [keep.tile([P, BANK], U32, name=f"x_codes{a}", align_bytes=64) for a in range(2)]
         cols = BANK // LIST_ROWS
         for a in range(2):
@@ -96,10 +96,10 @@ def tile_picked_hashprmslse_none_p_kernel(tc, x_words, x_scales, w1, gn, w2, off
                 x_codes[a][:], table_words[:].bitcast(U32).indirect(offs_sb[:, a * cols : (a + 1) * cols])
             )
 
-        w1_bf = keep.tile([P, H * PACK], BF16, name="w1_bf", align_bytes=64)
+        w1_bf = keep.tile([P, H * PACK], BF16, name="w1_bf", tag="w1_bf", align_bytes=64)
         deal_and_round(nc.scalar.copy, w1_bf, w1_raw[0][:], 0, 64)
-        deal_and_round(nc.scalar.copy, w1_bf, w1_raw[1][:, :, 0:176], 64, 108)
-        deal_and_round(nc.vector.tensor_copy, w1_bf, w1_raw[1][:, :, 176:256], 108, 128)
+        deal_and_round(nc.vector.tensor_copy, w1_bf, w1_raw[1][:], 64, 128, 0, 1)
+        deal_and_round(nc.scalar.copy, w1_bf, w1_raw[1][:], 64, 128, 1, PACK)
         w1_codes = [keep.tile([P, P], U32, name=f"w1_codes{t}", tag=f"w1_codes{t}", align_bytes=64) for t in range(PACK)]
         w1_scales = [keep.tile([P, P], U8, name=f"w1_scales{t}", align_bytes=64) for t in range(PACK)]
         sq = [keep.tile([P, S], F32, name=f"sq{t}") for t in range(PACK)]
@@ -108,25 +108,27 @@ def tile_picked_hashprmslse_none_p_kernel(tc, x_words, x_scales, w1, gn, w2, off
                 out=w1_codes[t][:].bitcast(FP8X4), scales=w1_scales[t][:], in_=w1_bf[:, t * BANK : (t + 1) * BANK]
             )
         for t in range(PACK):
-            for a in range(2):
-                y = psum.tile([P, BANK], F32, name="bank")
+            width = BANK // 2 if t == 0 else BANK
+            for s0 in range(0, S, width):
+                a, c0 = divmod(s0, BANK)
+                y = psum.tile([P, width], F32, name="bank")
                 nc.tensor.matmul_mx(
                     out=y[:],
                     lhsT=w1_codes[t][:].bitcast(FP8X4),
                     lhsT_scale=w1_scales[t][:],
-                    rhs=x_codes[a][:].bitcast(FP8X4),
-                    rhs_scale=x_scale_plane[:, a * BANK : (a + 1) * BANK],
+                    rhs=x_codes[a][:, c0 : c0 + width].bitcast(FP8X4),
+                    rhs_scale=x_scale_plane[:, s0 : s0 + width],
                     start=True,
                     stop=True,
                 )
                 nc.scalar.activation(
-                    sq[t][:, a * BANK : (a + 1) * BANK], y[:], ACT.Square, scale=gn_sb[:, t : t + 1]
+                    sq[t][:, s0 : s0 + width], y[:], ACT.Square, scale=gn_sb[:, t : t + 1]
                 )
 
-        w2_signed = keep.tile([P, PACK, N], BF16, name="w2_signed")
+        w2_signed = keep.tile([P, PACK, N], BF16, name="w2_signed", tag="w1_bf", align_bytes=64)
         for j in range(PACK):
             nc.vector.tensor_scalar(
-                w2_signed[:, j, :], w2_raw[j // 2][:, j % 2, :], gn_sign[:, j : j + 1], None, ALU.mult
+                w2_signed[:, j, :], w2_held[:, j * N : (j + 1) * N], gn_sign[:, j : j + 1], None, ALU.mult
             )
         w2_bf = keep.tile([P, N * PACK], BF16, name="w2_bf", tag="w1_codes3", align_bytes=64)
         deal_and_round(nc.scalar.copy, w2_bf, w2_signed[:], 0, 128)
@@ -226,9 +228,10 @@ def tile_picked_hashprmslse_none_p_kernel(tc, x_words, x_scales, w1, gn, w2, off
                 fetch_h(ahead)
             nc.vector.tensor_tensor(total[now][:], ex[now][:], ex_n2[now][:], ALU.add)
         out_rows = out.rearrange("(p t) v -> p t v", t=PACK)
-        for t in ORDER:
-            lse = ring.tile([P, V], F32, name="lse")
-            nc.scalar.activation(lse[:], total[t][:], ACT.Ln)
-            res = keep.tile([P, V], F32, name=f"res{t}")
-            nc.vector.tensor_tensor(res[:], lse[:], h_n3[t][:], ALU.subtract)
-            nc.sync.dma_start(out_rows[:, t, :], res[:])
+        pieces = [(t, slice(0, V)) for t in ORDER[:-1]] + [(ORDER[-1], v) for v, lc in halves]
+        for n, (t, v) in enumerate(pieces):
+            lse = keep.tile([P, v.stop - v.start], F32, name=f"lse{n}")
+            nc.scalar.activation(lse[:], total[t][:, v], ACT.Ln)
+            res = keep.tile([P, v.stop - v.start], F32, name=f"res{n}")
+            nc.vector.tensor_tensor(res[:], lse[:], h_n3[t][:, v], ALU.subtract)
+            nc.sync.dma_start(out_rows[:, t, v], res[:])

@@ -21,8 +21,8 @@ BANK = 512
 LIST_ROWS = 16
 PAIR_CHUNKS = ((0, 256), (256, 128), (384, 128))
 HALF = V // 2
-SCALAR_TILES = 3
-ORDER = (3, 0, 1, 2)
+SCALAR_TILES = 2
+ORDER = (0, 3, 2, 1)
 
 
 def deal_and_round(engine_copy, grouped, raw, m0, m1, t0=0, t1=PACK):
@@ -36,7 +36,7 @@ def tile_picked_hashprmslse_none_p_kernel(tc, x_words, x_scales, w1, gn, w2, off
     nc = tc.nc
     with ExitStack() as ctx:
         keep = ctx.enter_context(tc.tile_pool(name="keep", bufs=1))
-        ring = ctx.enter_context(tc.tile_pool(name="ring", bufs=3))
+        ring = ctx.enter_context(tc.tile_pool(name="ring", bufs=8))
         psum = ctx.enter_context(tc.psum_pool(name="psum", bufs=8))
 
         offs_sb = keep.tile([P, S // LIST_ROWS], U16, name="offs_sb")
@@ -81,20 +81,21 @@ def tile_picked_hashprmslse_none_p_kernel(tc, x_words, x_scales, w1, gn, w2, off
         picked_scales = keep.tile([P, S], U8, name="picked_scales")
         nc.vector.tensor_copy(picked_scales[:], table_scales[:].indirect(offs_sb[:]))
         for q in range(4):
-            nc.sync.dma_start(
+            nc.scalar.dma_start(
                 x_scale_plane[32 * q : 32 * q + 4, :].bitcast(I32),
                 picked_scales[32 * q : 32 * q + 32 : 8, :].bitcast(I32),
             )
-        w2_held = keep.tile([P, PACK * N], F32, name="w2_held", tag="table_scales")
-        w2_rows = w2.rearrange("(p j) c -> p (j c)", j=PACK)
-        for a in range(2):
-            nc.sync.dma_start(w2_held[:, 2 * a * N : 2 * (a + 1) * N], w2_rows[:, 2 * a * N : 2 * (a + 1) * N])
         x_codes = [keep.tile([P, BANK], U32, name=f"x_codes{a}", align_bytes=64) for a in range(2)]
         cols = BANK // LIST_ROWS
         for a in range(2):
             nc.vector.tensor_copy(
                 x_codes[a][:], table_words[:].bitcast(U32).indirect(offs_sb[:, a * cols : (a + 1) * cols])
             )
+
+        w2_held = keep.tile([P, PACK * N], F32, name="w2_held", tag="table_scales")
+        w2_rows = w2.rearrange("(p j) c -> p (j c)", j=PACK)
+        for a in range(2):
+            nc.scalar.dma_start(w2_held[:, 2 * a * N : 2 * (a + 1) * N], w2_rows[:, 2 * a * N : 2 * (a + 1) * N])
 
         w1_bf = keep.tile([P, H * PACK], BF16, name="w1_bf", tag="w1_bf", align_bytes=64)
         deal_and_round(nc.scalar.copy, w1_bf, w1_raw[0][:], 0, 64)
@@ -125,10 +126,10 @@ def tile_picked_hashprmslse_none_p_kernel(tc, x_words, x_scales, w1, gn, w2, off
                     sq[t][:, s0 : s0 + width], y[:], ACT.Square, scale=gn_sb[:, t : t + 1]
                 )
 
-        w2_signed = keep.tile([P, PACK, N], BF16, name="w2_signed", tag="w1_bf", align_bytes=64)
+        w2_signed = keep.tile([P, PACK, N], BF16, name="w2_signed")
         for j in range(PACK):
-            nc.vector.tensor_scalar(
-                w2_signed[:, j, :], w2_held[:, j * N : (j + 1) * N], gn_sign[:, j : j + 1], None, ALU.mult
+            nc.gpsimd.tensor_scalar(
+                w2_signed[:, j, :], w2_held[:, j * N : (j + 1) * N], gn_sign[:, j : j + 1], 0.0, ALU.mult, ALU.add
             )
         w2_bf = keep.tile([P, N * PACK], BF16, name="w2_bf", tag="w1_codes3", align_bytes=64)
         deal_and_round(nc.scalar.copy, w2_bf, w2_signed[:], 0, 128)
@@ -145,6 +146,8 @@ def tile_picked_hashprmslse_none_p_kernel(tc, x_words, x_scales, w1, gn, w2, off
             v0, width = PAIR_CHUNKS[c]
             if (c, t) == (2, 3):
                 lined[c, t] = keep.tile([P, 2 * width], F32, name="lined_last", tag="z_bf1", align_bytes=64)
+            elif (c, t) == (0, 3):
+                lined[c, t] = keep.tile([P, 2 * width], F32, name="lined_first", tag="ms1", align_bytes=64)
             else:
                 lined[c, t] = ring.tile([P, 2 * width], F32, name="lined")
             c0 = 2 * v0 // LIST_ROWS
@@ -157,9 +160,13 @@ def tile_picked_hashprmslse_none_p_kernel(tc, x_words, x_scales, w1, gn, w2, off
                     [P, PACK, width], F32, name=f"ms{c}", tag="z_bf0" if c == 2 else f"ms{c}", align_bytes=64
                 )
             pairs = lined[c, t][:].rearrange("p (v e) -> p v e", e=2)
-            nc.vector.scalar_tensor_tensor(
-                ms[c][:, t, :], pairs[:, :, 0], floor[:, t : t + 1], pairs[:, :, 1], ALU.add, ALU.add
-            )
+            if c == 0:
+                nc.gpsimd.tensor_tensor(ms[c][:, t, :], pairs[:, :, 0], pairs[:, :, 1], ALU.add)
+                nc.gpsimd.tensor_scalar(ms[c][:, t, :], ms[c][:, t, :], 1.0, floor[:, t : t + 1], ALU.mult, ALU.add)
+            else:
+                nc.vector.scalar_tensor_tensor(
+                    ms[c][:, t, :], pairs[:, :, 0], floor[:, t : t + 1], pairs[:, :, 1], ALU.add, ALU.add
+                )
 
         def root(c):
             width = PAIR_CHUNKS[c][1]
@@ -189,25 +196,33 @@ def tile_picked_hashprmslse_none_p_kernel(tc, x_words, x_scales, w1, gn, w2, off
             for t in ORDER:
                 copy(h_sb[t][:, v0 : v0 + width], h_banks[t][:, v0 : v0 + width])
 
-        steps = [(c, t) for c in range(len(PAIR_CHUNKS)) for t in range(PACK)]
-        line_up(*steps[0])
-        for now, ahead in zip(steps, steps[1:] + [None]):
-            if ahead == (2, 3):
-                second_product(1)
-            if ahead is not None:
-                line_up(*ahead)
-            if now == (2, 0):
-                nc.vector.quantize_mx(out=w2_codes[:].bitcast(FP8X4), scales=w2_scales[:], in_=w2_bf[:])
-                second_product(0)
-            add_pairs(*now)
-            if now[1] == PACK - 1:
-                root(now[0])
+        for t in range(PACK):
+            line_up(0, t)
+            add_pairs(0, t)
+        root(0)
+        for t in range(PACK):
+            line_up(1, t)
+        for t in range(PACK):
+            add_pairs(1, t)
+        root(1)
+        nc.vector.quantize_mx(out=w2_codes[:].bitcast(FP8X4), scales=w2_scales[:], in_=w2_bf[:])
+        line_up(2, 0)
+        second_product(0)
+        line_up(2, 1)
+        add_pairs(2, 0)
+        line_up(2, 2)
+        add_pairs(2, 1)
+        second_product(1)
+        line_up(2, 3)
+        add_pairs(2, 2)
+        add_pairs(2, 3)
+        root(2)
         second_product(2)
 
         ex = [keep.tile([P, V], F32, name=f"ex{t}") for t in range(PACK)]
-        ex_n2 = [keep.tile([P, V], F32, name=f"ex_n2_{t}") for t in range(PACK)]
-        h_n3 = [keep.tile([P, V], F32, name=f"h_n3_{t}") for t in range(PACK)]
-        total = [keep.tile([P, V], F32, name=f"total{t}") for t in range(PACK)]
+        ex_n2 = [keep.tile([P, V], F32, name=f"ex_n2_{t}", tag=f"ex_n2_{t}") for t in range(PACK)]
+        h_n3 = {}
+        total = {}
         half_cols = HALF // LIST_ROWS
         halves = [(slice(a * HALF, (a + 1) * HALF), slice(a * half_cols, (a + 1) * half_cols)) for a in range(2)]
         for t in ORDER:
@@ -216,19 +231,31 @@ def tile_picked_hashprmslse_none_p_kernel(tc, x_words, x_scales, w1, gn, w2, off
                 for v, lc in halves:
                     nc.scalar.activation(ex_n2[t][:, v], h_sb[t][:].indirect(n2_sb[:, lc]), ACT.Exp)
 
-        def fetch_h(t):
+        def fetch_h(t, tag):
+            h_n3[t] = keep.tile([P, V], F32, name=f"h_n3_{t}", tag=tag)
             for v, lc in halves:
                 nc.vector.tensor_copy(h_n3[t][:, v], h_sb[t][:].indirect(n3_sb[:, lc]))
 
-        fetch_h(3)
-        for v, lc in halves:
-            nc.vector.tensor_copy(ex_n2[3][:, v], ex[3][:].indirect(n2_sb[:, lc]))
-        for now, ahead in zip(ORDER, ORDER[1:] + (None,)):
-            if ahead is not None:
-                fetch_h(ahead)
-            nc.vector.tensor_tensor(total[now][:], ex[now][:], ex_n2[now][:], ALU.add)
+        def fetch_ex(t):
+            for v, lc in halves:
+                nc.vector.tensor_copy(ex_n2[t][:, v], ex[t][:].indirect(n2_sb[:, lc]))
+
+        def add_pair(t):
+            total[t] = keep.tile([P, V], F32, name=f"total{t}", tag="ex_n2_1" if t == 2 else f"total{t}")
+            (nc.vector if t == 2 else nc.gpsimd).tensor_tensor(total[t][:], ex[t][:], ex_n2[t][:], ALU.add)
+
+        fetch_h(0, "h_n3_0")
+        fetch_h(1, "h_n3_1")
+        add_pair(0)
+        fetch_ex(3)
+        fetch_ex(2)
+        add_pair(3)
+        add_pair(1)
+        fetch_h(3, "ex_n2_0")
+        fetch_h(2, "ex_n2_3")
+        add_pair(2)
         out_rows = out.rearrange("(p t) v -> p t v", t=PACK)
-        pieces = [(t, slice(0, V)) for t in ORDER[:-1]] + [(ORDER[-1], v) for v, lc in halves]
+        pieces = [(t, slice(0, V)) for t in (0, 3, 1)] + [(2, v) for v, lc in halves]
         for n, (t, v) in enumerate(pieces):
             lse = keep.tile([P, v.stop - v.start], F32, name=f"lse{n}")
             nc.scalar.activation(lse[:], total[t][:, v], ACT.Ln)

@@ -19,20 +19,28 @@ P = 128
 PACK = 4
 BANK = 512
 LIST_ROWS = 16
+BLOCK_ROWS = 8
+QUADRANT = 32
+EPS = 0.1
+
 PAIR_CHUNKS = ((0, 256), (256, 128), (384, 128))
-HALF = V // 2
-SCALAR_TILES = 2
-ORDER = (0, 3, 2, 1)
+GPSIMD_PAIR_TILES = 3
+SCALAR_TILES = (0, 1)
+VECTOR_TILES = (3, 2)
+H_ORDER = (SCALAR_TILES[0], *VECTOR_TILES, SCALAR_TILES[1])
+SUM_ORDER = (SCALAR_TILES[0], VECTOR_TILES[0], SCALAR_TILES[1], VECTOR_TILES[1])
 
 
-def deal_and_round(engine_copy, grouped, raw, m0, m1, t0=0, t1=PACK):
-    engine_copy(
+def deal_and_round(copy, grouped, raw, m0, m1, t0=0, t1=PACK):
+    copy(
         out=grouped[:].rearrange("p (t m j) -> p m j t", t=PACK, j=PACK)[:, m0:m1, :, t0:t1],
         in_=raw.rearrange("p j (m t) -> p m j t", t=PACK)[:, :, :, t0:t1],
     )
 
 
-def tile_picked_hashprmslse_none_p_kernel(tc, x_words, x_scales, w1, gn, w2, offs, n1, n2, n3, out):
+def tile_picked_hashprmslse_none_p_kernel(
+    tc, x_words, x_scales, w1, gn, w2, offs, n1, n2, n3, out
+):
     nc = tc.nc
     with ExitStack() as ctx:
         keep = ctx.enter_context(tc.tile_pool(name="keep", bufs=1))
@@ -44,8 +52,8 @@ def tile_picked_hashprmslse_none_p_kernel(tc, x_words, x_scales, w1, gn, w2, off
         n2_sb = keep.tile([P, V // LIST_ROWS], U16, name="n2_sb")
         n3_sb = keep.tile([P, V // LIST_ROWS], U16, name="n3_sb")
 
-        warm = keep.tile([P, 2], F32, name="warm")
-        nc.gpsimd.memset(warm[:, 0:1], 1.0)
+        one = keep.tile([P, 1], F32, name="one")
+        nc.gpsimd.memset(one[:], 1.0)
 
         table_scales = keep.tile([P, T], U8, name="table_scales", tag="table_scales")
         x_scale_plane = keep.tile([P, S], U8, name="x_scale_plane", align_bytes=64)
@@ -57,7 +65,8 @@ def tile_picked_hashprmslse_none_p_kernel(tc, x_words, x_scales, w1, gn, w2, off
 
         nc.sync.dma_start(offs_sb[:], offs)
         nc.sync.dma_start(
-            table_scales[:].bitcast(I32), x_scales[0].bitcast(I32).unsqueeze(1).to_broadcast([16, 8, T // 4])
+            table_scales[:].bitcast(I32),
+            x_scales[0].bitcast(I32).unsqueeze(1).to_broadcast([P // BLOCK_ROWS, BLOCK_ROWS, T // 4]),
         )
         nc.sync.dma_start(n1_sb[:], n1)
         nc.sync.dma_start(n2_sb[:], n2)
@@ -67,46 +76,52 @@ def tile_picked_hashprmslse_none_p_kernel(tc, x_words, x_scales, w1, gn, w2, off
         for a in range(2):
             nc.sync.dma_start(w1_raw[a][:], w1_rows[:, :, a * (H // 2) : (a + 1) * (H // 2)])
         nc.gpsimd.dma_start(gn_sb[:], gn.rearrange("(p t) o -> p (t o)", t=PACK))
-        nc.scalar.activation(warm[:, 1:2], warm[:, 0:1], ACT.Sqrt)
 
+        root_eps = keep.tile([P, 1], F32, name="root_eps")
+        nc.scalar.activation(root_eps[:], one[:], ACT.Sqrt, scale=EPS)
+
+        gn_root = keep.tile([P, PACK], F32, name="gn_root")
         floor = keep.tile([P, PACK], F32, name="floor")
-        gn_sq = keep.tile([P, PACK], F32, name="gn_sq")
-        nonneg = keep.tile([P, PACK], F32, name="nonneg")
+        twice_nonneg = keep.tile([P, PACK], F32, name="twice_nonneg")
         gn_sign = keep.tile([P, PACK], F32, name="gn_sign")
-        nc.gpsimd.tensor_tensor(gn_sq[:], gn_sb[:], gn_sb[:], ALU.mult)
-        nc.gpsimd.tensor_scalar(floor[:], gn_sq[:], 0.1, 0.0, ALU.mult, ALU.add)
-        nc.gpsimd.tensor_scalar(nonneg[:], gn_sb[:], 0.0, 2.0, ALU.is_ge, ALU.mult)
-        nc.gpsimd.tensor_scalar(gn_sign[:], nonneg[:], 1.0, -1.0, ALU.mult, ALU.add)
+        nc.gpsimd.tensor_scalar(gn_root[:], gn_sb[:], root_eps[:], 0.0, ALU.mult, ALU.add)
+        nc.gpsimd.tensor_tensor(floor[:], gn_root[:], gn_root[:], ALU.mult)
+        nc.gpsimd.tensor_scalar(twice_nonneg[:], gn_sb[:], 0.0, 2.0, ALU.is_ge, ALU.mult)
+        nc.gpsimd.tensor_scalar(gn_sign[:], twice_nonneg[:], 1.0, -1.0, ALU.mult, ALU.add)
 
         picked_scales = keep.tile([P, S], U8, name="picked_scales")
         nc.vector.tensor_copy(picked_scales[:], table_scales[:].indirect(offs_sb[:]))
-        for q in range(4):
+        for q0 in range(0, P, QUADRANT):
             nc.scalar.dma_start(
-                x_scale_plane[32 * q : 32 * q + 4, :].bitcast(I32),
-                picked_scales[32 * q : 32 * q + 32 : 8, :].bitcast(I32),
+                x_scale_plane[q0 : q0 + QUADRANT // BLOCK_ROWS, :].bitcast(I32),
+                picked_scales[q0 : q0 + QUADRANT : BLOCK_ROWS, :].bitcast(I32),
             )
         x_codes = [keep.tile([P, BANK], U32, name=f"x_codes{a}", align_bytes=64) for a in range(2)]
-        cols = BANK // LIST_ROWS
+        bank_cols = BANK // LIST_ROWS
         for a in range(2):
             nc.vector.tensor_copy(
-                x_codes[a][:], table_words[:].bitcast(U32).indirect(offs_sb[:, a * cols : (a + 1) * cols])
+                x_codes[a][:], table_words[:].bitcast(U32).indirect(offs_sb[:, a * bank_cols : (a + 1) * bank_cols])
             )
 
-        w2_held = keep.tile([P, PACK * N], F32, name="w2_held", tag="table_scales")
+        w2_raw = keep.tile([P, PACK * N], F32, name="w2_raw", tag="table_scales")
         w2_rows = w2.rearrange("(p j) c -> p (j c)", j=PACK)
         for a in range(2):
-            nc.scalar.dma_start(w2_held[:, 2 * a * N : 2 * (a + 1) * N], w2_rows[:, 2 * a * N : 2 * (a + 1) * N])
+            nc.scalar.dma_start(w2_raw[:, 2 * a * N : 2 * (a + 1) * N], w2_rows[:, 2 * a * N : 2 * (a + 1) * N])
 
         w1_bf = keep.tile([P, H * PACK], BF16, name="w1_bf", tag="w1_bf", align_bytes=64)
-        deal_and_round(nc.scalar.copy, w1_bf, w1_raw[0][:], 0, 64)
-        deal_and_round(nc.vector.tensor_copy, w1_bf, w1_raw[1][:], 64, 128, 0, 1)
-        deal_and_round(nc.scalar.copy, w1_bf, w1_raw[1][:], 64, 128, 1, PACK)
-        w1_codes = [keep.tile([P, P], U32, name=f"w1_codes{t}", tag=f"w1_codes{t}", align_bytes=64) for t in range(PACK)]
+        deal_and_round(nc.scalar.copy, w1_bf, w1_raw[0][:], 0, P // 2)
+        deal_and_round(nc.vector.tensor_copy, w1_bf, w1_raw[1][:], P // 2, P, 0, 1)
+        deal_and_round(nc.scalar.copy, w1_bf, w1_raw[1][:], P // 2, P, 1, PACK)
+        w1_codes = [
+            keep.tile([P, P], U32, name=f"w1_codes{t}", tag=f"w1_codes{t}", align_bytes=64) for t in range(PACK)
+        ]
         w1_scales = [keep.tile([P, P], U8, name=f"w1_scales{t}", align_bytes=64) for t in range(PACK)]
         sq = [keep.tile([P, S], F32, name=f"sq{t}") for t in range(PACK)]
         for t in range(PACK):
             nc.vector.quantize_mx(
-                out=w1_codes[t][:].bitcast(FP8X4), scales=w1_scales[t][:], in_=w1_bf[:, t * BANK : (t + 1) * BANK]
+                out=w1_codes[t][:].bitcast(FP8X4),
+                scales=w1_scales[t][:],
+                in_=w1_bf[:, t * P * PACK : (t + 1) * P * PACK],
             )
         for t in range(PACK):
             width = BANK // 2 if t == 0 else BANK
@@ -122,17 +137,15 @@ def tile_picked_hashprmslse_none_p_kernel(tc, x_words, x_scales, w1, gn, w2, off
                     start=True,
                     stop=True,
                 )
-                nc.scalar.activation(
-                    sq[t][:, s0 : s0 + width], y[:], ACT.Square, scale=gn_sb[:, t : t + 1]
-                )
+                nc.scalar.activation(sq[t][:, s0 : s0 + width], y[:], ACT.Square, scale=gn_sb[:, t : t + 1])
 
-        w2_signed = keep.tile([P, PACK, N], BF16, name="w2_signed")
+        w2_signed = keep.tile([P, PACK, N], BF16, name="w2_signed", tag="w1_bf", align_bytes=64)
         for j in range(PACK):
             nc.gpsimd.tensor_scalar(
-                w2_signed[:, j, :], w2_held[:, j * N : (j + 1) * N], gn_sign[:, j : j + 1], 0.0, ALU.mult, ALU.add
+                w2_signed[:, j, :], w2_raw[:, j * N : (j + 1) * N], gn_sign[:, j : j + 1], 0.0, ALU.mult, ALU.add
             )
-        w2_bf = keep.tile([P, N * PACK], BF16, name="w2_bf", tag="w1_codes3", align_bytes=64)
-        deal_and_round(nc.scalar.copy, w2_bf, w2_signed[:], 0, 128)
+        w2_bf = keep.tile([P, N * PACK], BF16, name="w2_bf", tag=f"w1_codes{PACK - 1}", align_bytes=64)
+        deal_and_round(nc.scalar.copy, w2_bf, w2_signed[:], 0, P)
         w2_codes = keep.tile([P, N], U32, name="w2_codes", align_bytes=64)
         w2_scales = keep.tile([P, N], U8, name="w2_scales", align_bytes=64)
 
@@ -142,38 +155,35 @@ def tile_picked_hashprmslse_none_p_kernel(tc, x_words, x_scales, w1, gn, w2, off
         lined = {}
         z_bf = {}
 
-        def line_up(c, t):
+        def line_up(c, t, tag=None):
             v0, width = PAIR_CHUNKS[c]
-            if (c, t) == (2, 3):
-                lined[c, t] = keep.tile([P, 2 * width], F32, name="lined_last", tag="z_bf1", align_bytes=64)
-            elif (c, t) == (0, 3):
-                lined[c, t] = keep.tile([P, 2 * width], F32, name="lined_first", tag="ms1", align_bytes=64)
-            else:
+            if tag is None:
                 lined[c, t] = ring.tile([P, 2 * width], F32, name="lined")
+            else:
+                lined[c, t] = keep.tile([P, 2 * width], F32, name=f"lined_{tag}", tag=tag, align_bytes=64)
             c0 = 2 * v0 // LIST_ROWS
             nc.vector.tensor_copy(lined[c, t][:], sq[t][:].indirect(n1_sb[:, c0 : c0 + 2 * width // LIST_ROWS]))
 
-        def add_pairs(c, t):
-            width = PAIR_CHUNKS[c][1]
-            if t == 0:
-                ms[c] = keep.tile(
-                    [P, PACK, width], F32, name=f"ms{c}", tag="z_bf0" if c == 2 else f"ms{c}", align_bytes=64
-                )
+        def open_sums(c, tag):
+            ms[c] = keep.tile([P, PACK, PAIR_CHUNKS[c][1]], F32, name=f"ms{c}", tag=tag, align_bytes=64)
+
+        def add_pairs_gpsimd(c, t):
             pairs = lined[c, t][:].rearrange("p (v e) -> p v e", e=2)
-            if c == 0:
-                nc.gpsimd.tensor_tensor(ms[c][:, t, :], pairs[:, :, 0], pairs[:, :, 1], ALU.add)
-                nc.gpsimd.tensor_scalar(ms[c][:, t, :], ms[c][:, t, :], 1.0, floor[:, t : t + 1], ALU.mult, ALU.add)
-            else:
-                nc.vector.scalar_tensor_tensor(
-                    ms[c][:, t, :], pairs[:, :, 0], floor[:, t : t + 1], pairs[:, :, 1], ALU.add, ALU.add
-                )
+            nc.gpsimd.tensor_tensor(ms[c][:, t, :], pairs[:, :, 0], pairs[:, :, 1], ALU.add)
+            nc.gpsimd.tensor_scalar(ms[c][:, t, :], ms[c][:, t, :], 1.0, floor[:, t : t + 1], ALU.mult, ALU.add)
+
+        def add_pairs_vector(c, t):
+            pairs = lined[c, t][:].rearrange("p (v e) -> p v e", e=2)
+            nc.vector.scalar_tensor_tensor(
+                ms[c][:, t, :], pairs[:, :, 0], floor[:, t : t + 1], pairs[:, :, 1], ALU.add, ALU.add
+            )
 
         def root(c):
             width = PAIR_CHUNKS[c][1]
             z_bf[c] = keep.tile([P, width * PACK], BF16, name=f"z_bf{c}", tag=f"z_bf{c}", align_bytes=64)
             nc.scalar.activation(
-                z_bf[c][:].rearrange("p (c i t) -> p c t i", i=4, t=PACK),
-                ms[c][:].rearrange("p t (c i) -> p c t i", i=4),
+                z_bf[c][:].rearrange("p (g e t) -> p g t e", e=4, t=PACK),
+                ms[c][:].rearrange("p t (g e) -> p g t e", e=4),
                 ACT.Sqrt,
             )
 
@@ -182,7 +192,7 @@ def tile_picked_hashprmslse_none_p_kernel(tc, x_words, x_scales, w1, gn, w2, off
             z_codes = keep.tile([P, width], U32, name=f"z_codes{c}", align_bytes=64)
             z_scales = keep.tile([P, width], U8, name=f"z_scales{c}", align_bytes=64)
             nc.vector.quantize_mx(out=z_codes[:].bitcast(FP8X4), scales=z_scales[:], in_=z_bf[c][:])
-            for t in ORDER:
+            for t in H_ORDER:
                 nc.tensor.matmul_mx(
                     out=h_banks[t][:, v0 : v0 + width],
                     lhsT=w2_codes[:, t * P : (t + 1) * P].bitcast(FP8X4),
@@ -192,73 +202,90 @@ def tile_picked_hashprmslse_none_p_kernel(tc, x_words, x_scales, w1, gn, w2, off
                     start=True,
                     stop=True,
                 )
-            copy = nc.scalar.copy if c + 1 < len(PAIR_CHUNKS) else nc.vector.tensor_copy
-            for t in ORDER:
+
+        def copy_h(c, copy):
+            v0, width = PAIR_CHUNKS[c]
+            for t in H_ORDER:
                 copy(h_sb[t][:, v0 : v0 + width], h_banks[t][:, v0 : v0 + width])
 
+        open_sums(0, "ms0")
         for t in range(PACK):
-            line_up(0, t)
-            add_pairs(0, t)
-        root(0)
+            line_up(0, t, tag="ms1" if t == GPSIMD_PAIR_TILES - 1 else None)
+            if t < GPSIMD_PAIR_TILES:
+                add_pairs_gpsimd(0, t)
         for t in range(PACK):
             line_up(1, t)
+        for t in range(GPSIMD_PAIR_TILES, PACK):
+            add_pairs_vector(0, t)
+        root(0)
+
+        line_up(2, 0)
+        open_sums(1, "ms1")
         for t in range(PACK):
-            add_pairs(1, t)
+            add_pairs_vector(1, t)
         root(1)
         nc.vector.quantize_mx(out=w2_codes[:].bitcast(FP8X4), scales=w2_scales[:], in_=w2_bf[:])
-        line_up(2, 0)
         second_product(0)
-        line_up(2, 1)
-        add_pairs(2, 0)
-        line_up(2, 2)
-        add_pairs(2, 1)
-        second_product(1)
-        line_up(2, 3)
-        add_pairs(2, 2)
-        add_pairs(2, 3)
-        root(2)
-        second_product(2)
+        copy_h(0, nc.scalar.copy)
 
+        open_sums(2, "z_bf0")
+        for t in range(1, PACK - 1):
+            line_up(2, t)
+            add_pairs_vector(2, t - 1)
+        second_product(1)
+        line_up(2, PACK - 1, tag="z_bf1")
+        for t in range(PACK - 2, PACK):
+            add_pairs_vector(2, t)
+        root(2)
+        copy_h(1, nc.vector.tensor_copy)
+        second_product(2)
+        copy_h(2, nc.vector.tensor_copy)
+
+        half_v = V // 2
+        half_cols = half_v // LIST_ROWS
+        halves = [(slice(a * half_v, (a + 1) * half_v), slice(a * half_cols, (a + 1) * half_cols)) for a in range(2)]
         ex = [keep.tile([P, V], F32, name=f"ex{t}") for t in range(PACK)]
         ex_n2 = [keep.tile([P, V], F32, name=f"ex_n2_{t}", tag=f"ex_n2_{t}") for t in range(PACK)]
         h_n3 = {}
         total = {}
-        half_cols = HALF // LIST_ROWS
-        halves = [(slice(a * HALF, (a + 1) * HALF), slice(a * half_cols, (a + 1) * half_cols)) for a in range(2)]
-        for t in ORDER:
+
+        for t in H_ORDER:
             nc.scalar.activation(ex[t][:], h_sb[t][:], ACT.Exp)
-            if t < SCALAR_TILES:
-                for v, lc in halves:
-                    nc.scalar.activation(ex_n2[t][:, v], h_sb[t][:].indirect(n2_sb[:, lc]), ACT.Exp)
+            if t in SCALAR_TILES:
+                for pairs_v, list_cols in halves:
+                    nc.scalar.activation(ex_n2[t][:, pairs_v], h_sb[t][:].indirect(n2_sb[:, list_cols]), ACT.Exp)
 
         def fetch_h(t, tag):
             h_n3[t] = keep.tile([P, V], F32, name=f"h_n3_{t}", tag=tag)
-            for v, lc in halves:
-                nc.vector.tensor_copy(h_n3[t][:, v], h_sb[t][:].indirect(n3_sb[:, lc]))
+            for pairs_v, list_cols in halves:
+                nc.vector.tensor_copy(h_n3[t][:, pairs_v], h_sb[t][:].indirect(n3_sb[:, list_cols]))
 
         def fetch_ex(t):
-            for v, lc in halves:
-                nc.vector.tensor_copy(ex_n2[t][:, v], ex[t][:].indirect(n2_sb[:, lc]))
+            for pairs_v, list_cols in halves:
+                nc.vector.tensor_copy(ex_n2[t][:, pairs_v], ex[t][:].indirect(n2_sb[:, list_cols]))
 
-        def add_pair(t):
-            total[t] = keep.tile([P, V], F32, name=f"total{t}", tag="ex_n2_1" if t == 2 else f"total{t}")
-            (nc.vector if t == 2 else nc.gpsimd).tensor_tensor(total[t][:], ex[t][:], ex_n2[t][:], ALU.add)
+        def add_ex(engine, t, tag):
+            total[t] = keep.tile([P, V], F32, name=f"total{t}", tag=tag)
+            engine.tensor_tensor(total[t][:], ex[t][:], ex_n2[t][:], ALU.add)
 
-        fetch_h(0, "h_n3_0")
-        fetch_h(1, "h_n3_1")
-        add_pair(0)
-        fetch_ex(3)
-        fetch_ex(2)
-        add_pair(3)
-        add_pair(1)
-        fetch_h(3, "ex_n2_0")
-        fetch_h(2, "ex_n2_3")
-        add_pair(2)
+        first, second, third, last = SUM_ORDER
+        for t in SCALAR_TILES:
+            fetch_h(t, f"h_n3_{t}")
+        add_ex(nc.gpsimd, first, f"total{first}")
+        for t in VECTOR_TILES:
+            fetch_ex(t)
+        add_ex(nc.gpsimd, second, f"total{second}")
+        add_ex(nc.gpsimd, third, f"total{third}")
+        fetch_h(second, f"ex_n2_{first}")
+        fetch_h(last, f"ex_n2_{second}")
+        add_ex(nc.vector, last, f"ex_n2_{third}")
+
         out_rows = out.rearrange("(p t) v -> p t v", t=PACK)
-        pieces = [(t, slice(0, V)) for t in (0, 3, 1)] + [(2, v) for v, lc in halves]
-        for n, (t, v) in enumerate(pieces):
-            lse = keep.tile([P, v.stop - v.start], F32, name=f"lse{n}")
-            nc.scalar.activation(lse[:], total[t][:, v], ACT.Ln)
-            res = keep.tile([P, v.stop - v.start], F32, name=f"res{n}")
-            nc.vector.tensor_tensor(res[:], lse[:], h_n3[t][:, v], ALU.subtract)
-            nc.sync.dma_start(out_rows[:, t, v], res[:])
+        pieces = [(t, slice(0, V)) for t in (first, second, third)] + [(last, pairs_v) for pairs_v, list_cols in halves]
+        for n, (t, pairs_v) in enumerate(pieces):
+            width = pairs_v.stop - pairs_v.start
+            lse = keep.tile([P, width], F32, name=f"lse{n}")
+            nc.scalar.activation(lse[:], total[t][:, pairs_v], ACT.Ln)
+            res = keep.tile([P, width], F32, name=f"res{n}")
+            nc.vector.tensor_tensor(res[:], lse[:], h_n3[t][:, pairs_v], ALU.subtract)
+            nc.sync.dma_start(out_rows[:, t, pairs_v], res[:])

from contextlib import ExitStack

import concourse.mybir as mybir

K, T, S, V, N, H = 512, 2048, 1024, 512, 512, 512
FLOPS = 2 * K * H * S + 2 * H * N * V

F32 = mybir.dt.float32
BF16 = mybir.dt.bfloat16
I32 = mybir.dt.int32
U32 = mybir.dt.uint32
U16 = mybir.dt.uint16
U8 = mybir.dt.uint8
FP8X4 = mybir.dt.float8_e4m3fn_x4
ACT = mybir.ActivationFunctionType
ALU = mybir.AluOpType

P = 128
PACK = 4
BANK = 512
LIST_ROWS = 16
BLOCK_ROWS = 8
QUADRANT = 32
EPS = 0.1

PAIR_CHUNKS = ((0, 256), (256, 128), (384, 128))
GPSIMD_PAIR_TILES = 3
SCALAR_TILES = (0, 1)
VECTOR_TILES = (3, 2)
H_ORDER = (SCALAR_TILES[0], *VECTOR_TILES, SCALAR_TILES[1])
SUM_ORDER = (SCALAR_TILES[0], VECTOR_TILES[0], SCALAR_TILES[1], VECTOR_TILES[1])


def deal_and_round(copy, grouped, raw, m0, m1, t0=0, t1=PACK):
    copy(
        out=grouped[:].rearrange("p (t m j) -> p m j t", t=PACK, j=PACK)[:, m0:m1, :, t0:t1],
        in_=raw.rearrange("p j (m t) -> p m j t", t=PACK)[:, :, :, t0:t1],
    )


def tile_picked_hashprmslse_none_p_kernel(
    tc, x_words, x_scales, w1, gn, w2, offs, n1, n2, n3, out
):
    nc = tc.nc
    with ExitStack() as ctx:
        keep = ctx.enter_context(tc.tile_pool(name="keep", bufs=1))
        ring = ctx.enter_context(tc.tile_pool(name="ring", bufs=8))
        psum = ctx.enter_context(tc.psum_pool(name="psum", bufs=8))

        offs_sb = keep.tile([P, S // LIST_ROWS], U16, name="offs_sb")
        n1_sb = keep.tile([P, S // LIST_ROWS], U16, name="n1_sb")
        n2_sb = keep.tile([P, V // LIST_ROWS], U16, name="n2_sb")
        n3_sb = keep.tile([P, V // LIST_ROWS], U16, name="n3_sb")

        one = keep.tile([P, 1], F32, name="one")
        nc.gpsimd.memset(one[:], 1.0)

        table_scales = keep.tile([P, T], U8, name="table_scales", tag="table_scales")
        x_scale_plane = keep.tile([P, S], U8, name="x_scale_plane", align_bytes=64)
        nc.gpsimd.memset(x_scale_plane[:].bitcast(I32), 0)

        table_words = keep.tile([P, T], I32, name="table_words")
        w1_raw = [keep.tile([P, PACK, H // 2], F32, name=f"w1_raw{a}") for a in range(2)]
        gn_sb = keep.tile([P, PACK], F32, name="gn_sb")

        nc.sync.dma_start(offs_sb[:], offs)
        nc.sync.dma_start(
            table_scales[:].bitcast(I32),
            x_scales[0].bitcast(I32).unsqueeze(1).to_broadcast([P // BLOCK_ROWS, BLOCK_ROWS, T // 4]),
        )
        nc.sync.dma_start(n1_sb[:], n1)
        nc.sync.dma_start(n2_sb[:], n2)
        nc.sync.dma_start(n3_sb[:], n3)
        nc.sync.dma_start(table_words[:], x_words[0].rearrange("p c r -> p (c r)").bitcast(I32))
        w1_rows = w1.rearrange("(p j) c -> p j c", j=PACK)
        for a in range(2):
            nc.sync.dma_start(w1_raw[a][:], w1_rows[:, :, a * (H // 2) : (a + 1) * (H // 2)])
        nc.gpsimd.dma_start(gn_sb[:], gn.rearrange("(p t) o -> p (t o)", t=PACK))

        root_eps = keep.tile([P, 1], F32, name="root_eps")
        nc.scalar.activation(root_eps[:], one[:], ACT.Sqrt, scale=EPS)

        gn_root = keep.tile([P, PACK], F32, name="gn_root")
        floor = keep.tile([P, PACK], F32, name="floor")
        twice_nonneg = keep.tile([P, PACK], F32, name="twice_nonneg")
        gn_sign = keep.tile([P, PACK], F32, name="gn_sign")
        nc.gpsimd.tensor_scalar(gn_root[:], gn_sb[:], root_eps[:], 0.0, ALU.mult, ALU.add)
        nc.gpsimd.tensor_tensor(floor[:], gn_root[:], gn_root[:], ALU.mult)
        nc.gpsimd.tensor_scalar(twice_nonneg[:], gn_sb[:], 0.0, 2.0, ALU.is_ge, ALU.mult)
        nc.gpsimd.tensor_scalar(gn_sign[:], twice_nonneg[:], 1.0, -1.0, ALU.mult, ALU.add)

        picked_scales = keep.tile([P, S], U8, name="picked_scales")
        nc.vector.tensor_copy(picked_scales[:], table_scales[:].indirect(offs_sb[:]))
        for q0 in range(0, P, QUADRANT):
            nc.scalar.dma_start(
                x_scale_plane[q0 : q0 + QUADRANT // BLOCK_ROWS, :].bitcast(I32),
                picked_scales[q0 : q0 + QUADRANT : BLOCK_ROWS, :].bitcast(I32),
            )
        x_codes = [keep.tile([P, BANK], U32, name=f"x_codes{a}", align_bytes=64) for a in range(2)]
        bank_cols = BANK // LIST_ROWS
        for a in range(2):
            nc.vector.tensor_copy(
                x_codes[a][:], table_words[:].bitcast(U32).indirect(offs_sb[:, a * bank_cols : (a + 1) * bank_cols])
            )

        w2_raw = keep.tile([P, PACK * N], F32, name="w2_raw", tag="table_scales")
        w2_rows = w2.rearrange("(p j) c -> p (j c)", j=PACK)
        for a in range(2):
            nc.scalar.dma_start(w2_raw[:, 2 * a * N : 2 * (a + 1) * N], w2_rows[:, 2 * a * N : 2 * (a + 1) * N])

        w1_bf = keep.tile([P, H * PACK], BF16, name="w1_bf", tag="w1_bf", align_bytes=64)
        deal_and_round(nc.scalar.copy, w1_bf, w1_raw[0][:], 0, P // 2)
        deal_and_round(nc.vector.tensor_copy, w1_bf, w1_raw[1][:], P // 2, P, 0, 1)
        deal_and_round(nc.scalar.copy, w1_bf, w1_raw[1][:], P // 2, P, 1, PACK)
        w1_codes = [
            keep.tile([P, P], U32, name=f"w1_codes{t}", tag=f"w1_codes{t}", align_bytes=64) for t in range(PACK)
        ]
        w1_scales = [keep.tile([P, P], U8, name=f"w1_scales{t}", align_bytes=64) for t in range(PACK)]
        sq = [keep.tile([P, S], F32, name=f"sq{t}") for t in range(PACK)]
        for t in range(PACK):
            nc.vector.quantize_mx(
                out=w1_codes[t][:].bitcast(FP8X4),
                scales=w1_scales[t][:],
                in_=w1_bf[:, t * P * PACK : (t + 1) * P * PACK],
            )
        for t in range(PACK):
            width = BANK // 2 if t == 0 else BANK
            for s0 in range(0, S, width):
                a, c0 = divmod(s0, BANK)
                y = psum.tile([P, width], F32, name="bank")
                nc.tensor.matmul_mx(
                    out=y[:],
                    lhsT=w1_codes[t][:].bitcast(FP8X4),
                    lhsT_scale=w1_scales[t][:],
                    rhs=x_codes[a][:, c0 : c0 + width].bitcast(FP8X4),
                    rhs_scale=x_scale_plane[:, s0 : s0 + width],
                    start=True,
                    stop=True,
                )
                nc.scalar.activation(sq[t][:, s0 : s0 + width], y[:], ACT.Square, scale=gn_sb[:, t : t + 1])

        w2_signed = keep.tile([P, PACK, N], BF16, name="w2_signed", tag="w1_bf", align_bytes=64)
        for j in range(PACK):
            nc.gpsimd.tensor_scalar(
                w2_signed[:, j, :], w2_raw[:, j * N : (j + 1) * N], gn_sign[:, j : j + 1], 0.0, ALU.mult, ALU.add
            )
        w2_bf = keep.tile([P, N * PACK], BF16, name="w2_bf", tag=f"w1_codes{PACK - 1}", align_bytes=64)
        deal_and_round(nc.scalar.copy, w2_bf, w2_signed[:], 0, P)
        w2_codes = keep.tile([P, N], U32, name="w2_codes", align_bytes=64)
        w2_scales = keep.tile([P, N], U8, name="w2_scales", align_bytes=64)

        h_banks = [psum.tile([P, V], F32, name="bank") for t in range(PACK)]
        h_sb = [keep.tile([P, V], F32, name=f"h_sb{t}") for t in range(PACK)]
        ms = {}
        lined = {}
        z_bf = {}

        def line_up(c, t, tag=None):
            v0, width = PAIR_CHUNKS[c]
            if tag is None:
                lined[c, t] = ring.tile([P, 2 * width], F32, name="lined")
            else:
                lined[c, t] = keep.tile([P, 2 * width], F32, name=f"lined_{tag}", tag=tag, align_bytes=64)
            c0 = 2 * v0 // LIST_ROWS
            nc.vector.tensor_copy(lined[c, t][:], sq[t][:].indirect(n1_sb[:, c0 : c0 + 2 * width // LIST_ROWS]))

        def open_sums(c, tag):
            ms[c] = keep.tile([P, PACK, PAIR_CHUNKS[c][1]], F32, name=f"ms{c}", tag=tag, align_bytes=64)

        def add_pairs_gpsimd(c, t):
            pairs = lined[c, t][:].rearrange("p (v e) -> p v e", e=2)
            nc.gpsimd.tensor_tensor(ms[c][:, t, :], pairs[:, :, 0], pairs[:, :, 1], ALU.add)
            nc.gpsimd.tensor_scalar(ms[c][:, t, :], ms[c][:, t, :], 1.0, floor[:, t : t + 1], ALU.mult, ALU.add)

        def add_pairs_vector(c, t):
            pairs = lined[c, t][:].rearrange("p (v e) -> p v e", e=2)
            nc.vector.scalar_tensor_tensor(
                ms[c][:, t, :], pairs[:, :, 0], floor[:, t : t + 1], pairs[:, :, 1], ALU.add, ALU.add
            )

        def root(c):
            width = PAIR_CHUNKS[c][1]
            z_bf[c] = keep.tile([P, width * PACK], BF16, name=f"z_bf{c}", tag=f"z_bf{c}", align_bytes=64)
            nc.scalar.activation(
                z_bf[c][:].rearrange("p (g e t) -> p g t e", e=4, t=PACK),
                ms[c][:].rearrange("p t (g e) -> p g t e", e=4),
                ACT.Sqrt,
            )

        def second_product(c):
            v0, width = PAIR_CHUNKS[c]
            z_codes = keep.tile([P, width], U32, name=f"z_codes{c}", align_bytes=64)
            z_scales = keep.tile([P, width], U8, name=f"z_scales{c}", align_bytes=64)
            nc.vector.quantize_mx(out=z_codes[:].bitcast(FP8X4), scales=z_scales[:], in_=z_bf[c][:])
            for t in H_ORDER:
                nc.tensor.matmul_mx(
                    out=h_banks[t][:, v0 : v0 + width],
                    lhsT=w2_codes[:, t * P : (t + 1) * P].bitcast(FP8X4),
                    lhsT_scale=w2_scales[:, t * P : (t + 1) * P],
                    rhs=z_codes[:].bitcast(FP8X4),
                    rhs_scale=z_scales[:],
                    start=True,
                    stop=True,
                )

        def copy_h(c, copy):
            v0, width = PAIR_CHUNKS[c]
            for t in H_ORDER:
                copy(h_sb[t][:, v0 : v0 + width], h_banks[t][:, v0 : v0 + width])

        open_sums(0, "ms0")
        for t in range(PACK):
            line_up(0, t, tag="ms1" if t == GPSIMD_PAIR_TILES - 1 else None)
            if t < GPSIMD_PAIR_TILES:
                add_pairs_gpsimd(0, t)
        for t in range(PACK):
            line_up(1, t)
        for t in range(GPSIMD_PAIR_TILES, PACK):
            add_pairs_vector(0, t)
        root(0)

        line_up(2, 0)
        open_sums(1, "ms1")
        for t in range(PACK):
            add_pairs_vector(1, t)
        root(1)
        nc.vector.quantize_mx(out=w2_codes[:].bitcast(FP8X4), scales=w2_scales[:], in_=w2_bf[:])
        second_product(0)
        copy_h(0, nc.scalar.copy)

        open_sums(2, "z_bf0")
        for t in range(1, PACK - 1):
            line_up(2, t)
            add_pairs_vector(2, t - 1)
        second_product(1)
        line_up(2, PACK - 1, tag="z_bf1")
        for t in range(PACK - 2, PACK):
            add_pairs_vector(2, t)
        root(2)
        copy_h(1, nc.vector.tensor_copy)
        second_product(2)
        copy_h(2, nc.vector.tensor_copy)

        half_v = V // 2
        half_cols = half_v // LIST_ROWS
        halves = [(slice(a * half_v, (a + 1) * half_v), slice(a * half_cols, (a + 1) * half_cols)) for a in range(2)]
        ex = [keep.tile([P, V], F32, name=f"ex{t}") for t in range(PACK)]
        ex_n2 = [keep.tile([P, V], F32, name=f"ex_n2_{t}", tag=f"ex_n2_{t}") for t in range(PACK)]
        h_n3 = {}
        total = {}

        for t in H_ORDER:
            nc.scalar.activation(ex[t][:], h_sb[t][:], ACT.Exp)
            if t in SCALAR_TILES:
                for pairs_v, list_cols in halves:
                    nc.scalar.activation(ex_n2[t][:, pairs_v], h_sb[t][:].indirect(n2_sb[:, list_cols]), ACT.Exp)

        def fetch_h(t, tag):
            h_n3[t] = keep.tile([P, V], F32, name=f"h_n3_{t}", tag=tag)
            for pairs_v, list_cols in halves:
                nc.vector.tensor_copy(h_n3[t][:, pairs_v], h_sb[t][:].indirect(n3_sb[:, list_cols]))

        def fetch_ex(t):
            for pairs_v, list_cols in halves:
                nc.vector.tensor_copy(ex_n2[t][:, pairs_v], ex[t][:].indirect(n2_sb[:, list_cols]))

        def add_ex(engine, t, tag):
            total[t] = keep.tile([P, V], F32, name=f"total{t}", tag=tag)
            engine.tensor_tensor(total[t][:], ex[t][:], ex_n2[t][:], ALU.add)

        first, second, third, last = SUM_ORDER
        for t in SCALAR_TILES:
            fetch_h(t, f"h_n3_{t}")
        add_ex(nc.gpsimd, first, f"total{first}")
        for t in VECTOR_TILES:
            fetch_ex(t)
        add_ex(nc.gpsimd, second, f"total{second}")
        add_ex(nc.gpsimd, third, f"total{third}")
        fetch_h(second, f"ex_n2_{first}")
        fetch_h(last, f"ex_n2_{second}")
        add_ex(nc.vector, last, f"ex_n2_{third}")

        out_rows = out.rearrange("(p t) v -> p t v", t=PACK)
        pieces = [(t, slice(0, V)) for t in (first, second, third)] + [(last, pairs_v) for pairs_v, list_cols in halves]
        for n, (t, pairs_v) in enumerate(pieces):
            width = pairs_v.stop - pairs_v.start
            lse = keep.tile([P, width], F32, name=f"lse{n}")
            nc.scalar.activation(lse[:], total[t][:, pairs_v], ACT.Ln)
            res = keep.tile([P, width], F32, name=f"res{n}")
            nc.vector.tensor_tensor(res[:], lse[:], h_n3[t][:, pairs_v], ALU.subtract)
            nc.sync.dma_start(out_rows[:, t, pairs_v], res[:])
